import numpy as np, ml_dtypes
CORES = [0,1,2,3]
N = 4
def setup_inputs(rng):
    return {"x": rng.standard_normal((N, 128, 16), dtype=np.float32).astype(ml_dtypes.bfloat16)}
def reference(x):
    s = x.max(axis=0)
    return {"y": np.broadcast_to(s, (N,) + s.shape)}

@@ -1,0 +1,55 @@
+from concourse.bass import DstId, RemoteDMATransfer
+
+HELPER = 4
+W = 16
+ENGINES = 16
+ALU_MAX = 2
+
+SCRATCH = {
+    "xs": ("sbuf", [128, W], "bfloat16"),
+    "gather": ("sbuf", [128, 4 * W], "bfloat16"),
+    "res": ("sbuf", [128, W], "bfloat16"),
+}
+SEMAPHORES = ["loaded", "arrived", "sent", "folded", "stored"]
+
+
+def rank_program(g, core, T, topo):
+    rank = T.rank_of(core)
+    n = len(T.cores)
+
+    if core == HELPER:
+        g.wait_ge(T.sem.arrived, n * ENGINES)
+        ids = []
+        for c in T.cores:
+            rid, pid, _se = topo.addr(c)
+            ids.append(DstId(rid=rid, pnc=pid))
+        g.remote_dma_fused(
+            [RemoteDMATransfer(
+                dst_ids=ids,
+                dma_engine_mask=0xFFFF,
+                remote_sem=T.sem.folded,
+                srcs=[T.gather[:, r * W:(r + 1) * W] for r in range(n)],
+                dsts=[T.res[:] for _c in T.cores],
+                alu_op=ALU_MAX,
+            )],
+            local_sem=T.sem.sent,
+        )
+        g.wait_ge(T.sem.sent, ENGINES)
+        return
+
+    if rank is None:
+        return
+
+    g.dma_start(T.xs[:], T.x[:]).then_inc(T.sem.loaded, 16)
+    g.wait_ge(T.sem.loaded, 16)
+
+    rid, pid, _se = topo.addr(HELPER)
+    g.remote_dma(
+        T.gather[:, rank * W:(rank + 1) * W], T.xs[:],
+        T.sem.arrived, T.sem.sent, pid, rid, topo.mask(core, HELPER),
+    )
+    g.wait_ge(T.sem.sent, ENGINES)
+
+    g.wait_ge(T.sem.folded, ENGINES)
+    g.dma_start(T.y[:], T.res[:]).then_inc(T.sem.stored, 16)
+    g.wait_ge(T.sem.stored, 16)

@@ -21,15 +21,15 @@ def rank_program(g, core, T, topo):
         g.wait_ge(T.sem.arrived, n * ENGINES)
         ids = []
         for c in T.cores:
-            rid, pid, _se = topo.addr(c)
-            ids.append(DstId(rid=rid, pnc=pid))
+            a = topo.addr(c)
+            ids.append(DstId(rid=a[0], pnc=a[1]))
         g.remote_dma_fused(
             [RemoteDMATransfer(
                 dst_ids=ids,
                 dma_engine_mask=0xFFFF,
                 remote_sem=T.sem.folded,
                 srcs=[T.gather[:, r * W:(r + 1) * W] for r in range(n)],
-                dsts=[T.res[:] for _c in T.cores],
+                dsts=[T.res[:] for c in T.cores],
                 alu_op=ALU_MAX,
             )],
             local_sem=T.sem.sent,
@@ -43,10 +43,10 @@ def rank_program(g, core, T, topo):
     g.dma_start(T.xs[:], T.x[:]).then_inc(T.sem.loaded, 16)
     g.wait_ge(T.sem.loaded, 16)
 
-    rid, pid, _se = topo.addr(HELPER)
+    a = topo.addr(HELPER)
     g.remote_dma(
         T.gather[:, rank * W:(rank + 1) * W], T.xs[:],
-        T.sem.arrived, T.sem.sent, pid, rid, topo.mask(core, HELPER),
+        T.sem.arrived, T.sem.sent, a[1], a[0], topo.mask(core, HELPER),
     )
     g.wait_ge(T.sem.sent, ENGINES)
 

from concourse.bass import DstId, RemoteDMATransfer

HELPER = 4
W = 16
ENGINES = 16
ALU_MAX = 2

SCRATCH = {
    "xs": ("sbuf", [128, W], "bfloat16"),
    "gather": ("sbuf", [128, 4 * W], "bfloat16"),
    "res": ("sbuf", [128, W], "bfloat16"),
}
SEMAPHORES = ["loaded", "arrived", "sent", "folded", "stored"]


def rank_program(g, core, T, topo):
    rank = T.rank_of(core)
    n = len(T.cores)

    if core == HELPER:
        g.wait_ge(T.sem.arrived, n * ENGINES)
        ids = []
        for c in T.cores:
            a = topo.addr(c)
            ids.append(DstId(rid=a[0], pnc=a[1]))
        g.remote_dma_fused(
            [RemoteDMATransfer(
                dst_ids=ids,
                dma_engine_mask=0xFFFF,
                remote_sem=T.sem.folded,
                srcs=[T.gather[:, r * W:(r + 1) * W] for r in range(n)],
                dsts=[T.res[:] for c in T.cores],
                alu_op=ALU_MAX,
            )],
            local_sem=T.sem.sent,
        )
        g.wait_ge(T.sem.sent, ENGINES)
        return

    if rank is None:
        return

    g.dma_start(T.xs[:], T.x[:]).then_inc(T.sem.loaded, 16)
    g.wait_ge(T.sem.loaded, 16)

    a = topo.addr(HELPER)
    g.remote_dma(
        T.gather[:, rank * W:(rank + 1) * W], T.xs[:],
        T.sem.arrived, T.sem.sent, a[1], a[0], topo.mask(core, HELPER),
    )
    g.wait_ge(T.sem.sent, ENGINES)

    g.wait_ge(T.sem.folded, ENGINES)
    g.dma_start(T.y[:], T.res[:]).then_inc(T.sem.stored, 16)
    g.wait_ge(T.sem.stored, 16)
